import numpy as np
import ml_dtypes


def mxq(x, axis, fmt="e4m3"):
    dtype, down = {"e4m3": (ml_dtypes.float8_e4m3fn, 7), "e5m2": (ml_dtypes.float8_e5m2, 14)}[fmt]
    v = np.moveaxis(np.asarray(x, np.float32).astype(ml_dtypes.bfloat16).astype(np.float64), axis, -1)
    blocks = v.reshape(v.shape[:-1] + (-1, 32))
    amax = np.abs(blocks).max(-1, keepdims=True)
    byte = np.maximum(np.where(amax > 0, np.frexp(amax)[1] - 1 + 127, 0) - down, 1)
    scale = np.exp2(byte - 127.0)
    codes = (blocks / scale).astype(np.float32).astype(dtype).astype(np.float64)
    return np.moveaxis((codes * scale).reshape(v.shape), -1, axis)


WIDE = False


def mx_kscale(k):
    if not WIDE:
        return np.ones(k)
    levels = np.array([10, -10, 5, -5, 0])
    if k % 512:
        return np.exp2(np.random.permutation(np.resize(levels, k // 32))).repeat(32)
    a = np.empty((k // 512, 16))
    for p in range(k // 512):
        a[p, :8] = np.random.permutation(np.resize(levels, 8))
        for g in range(8):
            far = levels[np.abs(levels - a[p, g]) >= 10]
            a[p, g + 8] = far[np.random.randint(len(far))]
    return np.exp2(a.ravel()).repeat(32)


def f64(x):
    return np.asarray(x).astype(np.float64)


def striped(idx):
    return np.tile(np.asarray(idx).reshape(-1, 16).T, (8, 1)).astype(np.uint16)


def unstriped(offs):
    return offs[:16].T.reshape(-1).astype(np.int64)


E2M1 = np.array([0.0, 0.5, 1.0, 1.5, 2.0, 3.0, 4.0, 6.0, -0.0, -0.5, -1.0, -1.5, -2.0, -3.0, -4.0, -6.0])


def pack_weight(w, fmt):
    k, n = w.shape
    w = f64(np.asarray(w, np.float32).astype(ml_dtypes.bfloat16)).reshape(k // 32, 32, n)
    amax = np.abs(w).max(1)
    if fmt == "e4m3":
        byte = np.frexp(amax)[1] - 1 + 127 - 7
    else:
        mant, ex = np.frexp(amax / 6.0)
        byte = np.where(mant > 0.5, ex, ex - 1) + 127
    byte = np.clip(np.where(amax > 0, byte, 1), 1, 254)
    scaled = (w * np.exp2(127.0 - byte)[:, None, :]).reshape(k, n).astype(np.float32)
    by_word = np.ascontiguousarray(scaled.reshape(k // 512, 128, 4, n).transpose(0, 1, 3, 2))
    if fmt == "e4m3":
        words = by_word.astype(ml_dtypes.float8_e4m3fn).view(np.uint8)
    else:
        c = by_word.astype(ml_dtypes.float4_e2m1fn).view(np.uint8) & 0xF
        words = (c[..., 0::2] | (c[..., 1::2] << 4)).reshape(k // 512, 128, 2 * n)
    return np.ascontiguousarray(words), np.ascontiguousarray(byte.astype(np.uint8).reshape(k // 512, 16, n))


def unpack_weight(words, scales, fmt):
    g, _, n = scales.shape
    words = np.ascontiguousarray(words).reshape(g, 128, n, -1)
    if fmt == "e4m3":
        vals = words.view(ml_dtypes.float8_e4m3fn).astype(np.float64)
    else:
        nib = np.empty((g, 128, n, 4), np.uint8)
        nib[..., 0::2] = words & 0xF
        nib[..., 1::2] = words >> 4
        vals = E2M1[nib]
    vals = vals * np.repeat(np.exp2(scales.astype(np.float64) - 127.0), 8, axis=1)[..., None]
    return vals.transpose(0, 1, 3, 2).reshape(g * 512, n)


D, T, I, J, Q = 512, 4096, 512, 512, 128


def setup_inputs():
    n = np.random.standard_normal
    idx = np.random.permutation(T)[:I]
    idx2 = np.random.permutation(T)[:J]
    fd = mx_kscale(D)
    vocp = pack_weight(n((D, T)) / fd[:, None], "e4m3")
    return {
        "hid": (n((D, Q)) * 1.0 / np.sqrt(D) * fd[:, None]).astype(np.float32),
        "voc_words": vocp[0],
        "voc_scales": vocp[1],
        "lfreq": np.tile(np.random.uniform(-9.0, -5.0, T), (128, 1)).astype(np.float32),
        "tb": (np.random.uniform(-0.5, 0.5, (1, I))).astype(np.float32),
        "offs": striped(idx),
        "offs2": striped(idx2),
    }


def reference(hid, voc_words, voc_scales, lfreq, tb, offs, offs2):
    idx = unstriped(offs)
    idx2 = unstriped(offs2)
    vocu = unpack_weight(voc_words, voc_scales, "e4m3")
    hidq = mxq(f64(hid), 0, "e4m3")
    vocidxg = vocu[:, idx]
    a = hidq.T @ vocidxg
    vocidx2g = vocu[:, idx2]
    b = hidq.T @ vocidx2g
    r = b - f64(lfreq)[:1][:, idx2]
    m1 = np.max(r, axis=1, keepdims=True)
    z = np.log(np.sum(np.exp(r - m1), axis=1, keepdims=True)) + m1
    y = a + f64(tb) - z + 12.0
    return y

@@ -1,0 +1,138 @@
+import math
+from contextlib import ExitStack
+
+import concourse.mybir as mybir
+from concourse.masks import make_identity
+
+D, T, NI, NJ, Q = 512, 4096, 512, 512, 128
+P = 128
+PACK = 4
+FLOPS = 2 * Q * D * (NI + NJ)
+BYTES = D * T + (D // 32) * T + 4 * D * Q + 4 * T + 4 * NI + 2 * 2 * P * 32 + 4 * Q * NI
+
+F32 = mybir.dt.float32
+BF16 = mybir.dt.bfloat16
+I32 = mybir.dt.int32
+U32 = mybir.dt.uint32
+U16 = mybir.dt.uint16
+U8 = mybir.dt.uint8
+FP8X4 = mybir.dt.float8_e4m3fn_x4
+ALU = mybir.AluOpType
+ACT = mybir.ActivationFunctionType
+AX = mybir.AxisListType
+
+TERMS = 24
+EXP_MASK = 0x7F800000
+MANT = 0x280000
+MANT_VALUE = 1.3125
+FLIP = (0x80000000 | EXP_MASK | MANT) - (1 << 32)
+BITS_OF_ONE = (0x80000000 | (127 << 23) | MANT) - (1 << 32)
+LF_ROW = P - 1
+
+
+def tile_attend_sampledsum_kernel(tc, hid, voc_words, voc_scales, lfreq, tb, offs, offs2, out):
+    nc = tc.nc
+    with ExitStack() as ctx:
+        sb = ctx.enter_context(tc.tile_pool(name="sb", bufs=1))
+        ps = ctx.enter_context(tc.psum_pool(name="ps", bufs=1))
+
+        o2 = sb.tile([P, NJ // 16], U16, name="o2")
+        o1 = sb.tile([P, NI // 16], U16, name="o1")
+        words = sb.tile([P, T], I32, name="words", align_bytes=64)
+        scales = sb.tile([P, T], U8, name="scales", align_bytes=64)
+        lf = sb.tile([P, T], F32, name="lf", tag="lf", align_bytes=64)
+        hraw = sb.tile([P, PACK, Q], F32, name="hraw")
+        tbcol = sb.tile([P, 4], F32, name="tbcol")
+
+        nc.vector.memset(scales[:].bitcast(I32), 0)
+        nc.vector.memset(lf[0:LF_ROW, :], 0.0)
+
+        nc.sync.dma_start(o2[:], offs2)
+        nc.sync.dma_start(o1[:], offs)
+        nc.sync.dma_start(out=lf[LF_ROW:P, :], in_=lfreq[0:1, :])
+        nc.sync.dma_start(out=hraw[:], in_=hid.rearrange("(p j) q -> p j q", j=PACK))
+        nc.sync.dma_start(out=tbcol[:], in_=tb.rearrange("o (k c) -> (o k) c", c=4))
+        nc.sync.dma_start(out=words[:], in_=voc_words[0].rearrange("p n t -> p (n t)").bitcast(I32))
+        for g in range(4):
+            nc.scalar.dma_start(
+                out=scales[32 * g : 32 * g + 4, :].bitcast(I32),
+                in_=voc_scales[0, 4 * g : 4 * g + 4, :].bitcast(I32),
+            )
+
+        ident = sb.tile([P, P], F32, name="ident")
+        make_identity(nc, ident[:])
+
+        kf = sb.tile([P, TERMS], F32, name="kf")
+        ke = sb.tile([P, TERMS], I32, name="ke")
+        pw = sb.tile([P, TERMS], I32, name="pw")
+        den = sb.tile([P, TERMS], F32, name="den")
+        cf = sb.tile([P, TERMS + 1], F32, name="cf")
+        nc.gpsimd.iota(kf[:], [[-1, TERMS]], base=TERMS, channel_multiplier=0, allow_small_or_imprecise_dtypes=True)
+        nc.gpsimd.iota(ke[:], [[-2, TERMS]], base=127 + 2 * TERMS, channel_multiplier=0)
+        nc.vector.tensor_scalar(pw[:], ke[:], 23, None, ALU.logical_shift_left)
+        nc.vector.tensor_tensor(den[:], kf[:], pw[:].bitcast(F32), ALU.mult)
+        nc.vector.reciprocal(cf[:, 0:TERMS], den[:])
+
+        hgrp = sb.tile([P, Q, PACK], BF16, name="hgrp", align_bytes=64)
+        hq = sb.tile([P, Q], U32, name="hq", align_bytes=64)
+        hs = sb.tile([P, Q], U8, name="hs", align_bytes=64)
+        nc.scalar.copy(hgrp[:], hraw[:].rearrange("p j q -> p q j"))
+
+        gs1 = sb.tile([P, NI], U8, name="gs1", align_bytes=64)
+        gw2 = sb.tile([P, NJ], U32, name="gw2", align_bytes=64)
+        gw1 = sb.tile([P, NI], U32, name="gw1", align_bytes=64)
+        lfg = sb.tile([P, NJ], F32, name="lfg")
+        nc.vector.tensor_copy(lfg[:], lf[:].indirect(o2[:]))
+        gs2 = sb.tile([P, NJ], U8, name="gs2", tag="lf", align_bytes=64)
+        nc.vector.tensor_copy(gs2[:], scales[:].indirect(o2[:]))
+        nc.vector.quantize_mx(out=hq[:].bitcast(FP8X4), scales=hs[:], in_=hgrp[:].rearrange("p q j -> p (q j)"))
+        nc.vector.tensor_copy(gs1[:], scales[:].indirect(o1[:]))
+        nc.vector.tensor_copy(gw2[:], words[:].bitcast(U32).indirect(o2[:]))
+        nc.vector.tensor_copy(gw1[:], words[:].bitcast(U32).indirect(o1[:]))
+
+        lft = ps.tile([P, 4, P], F32, name="lft")
+        lfcol = sb.tile([P, 4], F32, name="lfcol")
+        lfp = ps.tile([P, 4, P], F32, name="lfp")
+        lfb = sb.tile([P, NJ], F32, name="lfb")
+        for c in range(4):
+            nc.tensor.transpose(lft[:, c, :], lfg[:, c * P : (c + 1) * P], ident[:])
+        nc.scalar.copy(lfcol[:], lft[:, :, LF_ROW])
+        for c in range(4):
+            nc.tensor.transpose(lfp[:, c, :], lfcol[:, c : c + 1].to_broadcast([P, P]), ident[:])
+        nc.scalar.copy(lfb[:], lfp[:].rearrange("p c k -> p (c k)"))
+
+        tbp = ps.tile([P, 4, P], F32, name="tbp")
+        tbb = sb.tile([P, P, 4], F32, name="tbb")
+        for c in range(4):
+            nc.tensor.transpose(tbp[:, c, :], tbcol[:, c : c + 1].to_broadcast([P, P]), ident[:])
+        nc.scalar.copy(tbb[:], tbp[:].rearrange("p c k -> p k c"))
+
+        pb = ps.tile([P, NJ], F32, name="pb")
+        pa = ps.tile([P, NI], F32, name="pa")
+        nc.tensor.matmul_mx(out=pb[:], lhsT=hq[:].bitcast(FP8X4), lhsT_scale=hs[:],
+                            rhs=gw2[:].bitcast(FP8X4), rhs_scale=gs2[:], start=True, stop=True)
+        nc.tensor.matmul_mx(out=pa[:], lhsT=hq[:].bitcast(FP8X4), lhsT_scale=hs[:],
+                            rhs=gw1[:].bitcast(FP8X4), rhs_scale=gs1[:], start=True, stop=True)
+
+        nr = sb.tile([P, NJ], F32, name="nr")
+        negm = sb.tile([P, 1], F32, name="negm")
+        ex = sb.tile([P, NJ], F32, name="ex")
+        ssum = sb.tile([P, 1], F32, name="ssum")
+        nc.vector.tensor_tensor(nr[:], lfb[:], pb[:], ALU.subtract)
+        nc.vector.tensor_reduce(negm[:], nr[:], AX.X, ALU.min)
+        nc.scalar.activation(ex[:], nr[:], ACT.Exp, bias=negm[:], scale=-1.0, accum_out=ssum[:])
+
+        at = sb.tile([P, NI], F32, name="at")
+        nc.vector.scalar_tensor_tensor(at[:], pa[:], negm[:], tbb[:].rearrange("p k c -> p (k c)"), ALU.add, ALU.add)
+
+        inv = sb.tile([P, 1], I32, name="inv")
+        w = sb.tile([P, TERMS + 1], F32, name="w")
+        hor = sb.tile([P, TERMS + 1], F32, name="hor")
+        nc.vector.tensor_scalar(inv[:], ssum[:].bitcast(I32), EXP_MASK, FLIP, ALU.bitwise_and, ALU.bitwise_xor)
+        nc.vector.tensor_scalar(w[:], ssum[:].to_broadcast([P, TERMS + 1]), inv[:].bitcast(F32), 4.0, ALU.mult, ALU.add)
+        nc.vector.tensor_scalar(cf[:, TERMS : TERMS + 1], inv[:], float(-BITS_OF_ONE), math.log(2.0) / (1 << 23), ALU.add, ALU.mult)
+        nc.vector.tensor_tensor_scan(hor[:], w[:], cf[:], 0.0, ALU.mult, ALU.add)
+
+        res = sb.tile([P, NI], F32, name="res")
+        nc.vector.tensor_scalar(res[:], at[:], hor[:, TERMS : TERMS + 1], 12.0 + math.log(MANT_VALUE / 4.0), ALU.add, ALU.add)
+        nc.sync.dma_start(out=out, in_=res[:])

@@ -28,6 +28,9 @@ MANT_VALUE = 1.3125
 FLIP = (0x80000000 | EXP_MASK | MANT) - (1 << 32)
 BITS_OF_ONE = (0x80000000 | (127 << 23) | MANT) - (1 << 32)
 LF_ROW = P - 1
+SPLIT = 1600
+SC_ROW = 48
+VCOLS = 320
 
 
 def tile_attend_sampledsum_kernel(tc, hid, voc_words, voc_scales, lfreq, tb, offs, offs2, out):
@@ -39,61 +42,65 @@ def tile_attend_sampledsum_kernel(tc, hid, voc_words, voc_scales, lfreq, tb, off
         o2 = sb.tile([P, NJ // 16], U16, name="o2")
         o1 = sb.tile([P, NI // 16], U16, name="o1")
         words = sb.tile([P, T], I32, name="words", align_bytes=64)
-        scales = sb.tile([P, T], U8, name="scales", align_bytes=64)
+        scales = sb.tile([P, T], U8, name="scales", tag="scales", align_bytes=64)
         lf = sb.tile([P, T], F32, name="lf", tag="lf", align_bytes=64)
         hraw = sb.tile([P, PACK, Q], F32, name="hraw")
         tbcol = sb.tile([P, 4], F32, name="tbcol")
 
-        nc.vector.memset(scales[:].bitcast(I32), 0)
-        nc.vector.memset(lf[0:LF_ROW, :], 0.0)
+        scw = scales[:].bitcast(I32)
+        ident = sb.tile([P, P], F32, name="ident")
+        ke = sb.tile([P, TERMS], I32, name="ke")
+        pl2 = sb.tile([P, NJ], U8, name="pl2", align_bytes=64)
+        pl1 = sb.tile([P, NI], U8, name="pl1", align_bytes=64)
+        nc.gpsimd.memset(scw[64:P, :], 0)
+        nc.vector.memset(scw[0:SC_ROW, 0 : T // 4 - 1], 0)
+        nc.vector.memset(scw[0:SC_ROW, T // 4 - 1 : T // 4], 0)
+        nc.vector.memset(lf[0:LF_ROW, 0 : SPLIT - 1], 0.0)
+        nc.vector.memset(lf[0:LF_ROW, SPLIT - 1 : SPLIT], 0.0)
+        nc.gpsimd.memset(lf[0:LF_ROW, SPLIT:T], 0.0)
+        make_identity(nc, ident[:])
+        nc.gpsimd.memset(pl2[:].bitcast(I32), 0)
+        nc.gpsimd.memset(pl1[:].bitcast(I32), 0)
+        nc.gpsimd.iota(ke[:], [[-2, TERMS]], base=126 + 2 * TERMS, channel_multiplier=0)
 
         nc.sync.dma_start(o2[:], offs2)
+        nc.sync.dma_start(out=scw[SC_ROW : SC_ROW + 16, :], in_=voc_scales[0].bitcast(I32))
+        nc.sync.dma_start(out=hraw[:], in_=hid.rearrange("(p j) q -> p j q", j=PACK))
         nc.sync.dma_start(o1[:], offs)
         nc.sync.dma_start(out=lf[LF_ROW:P, :], in_=lfreq[0:1, :])
-        nc.sync.dma_start(out=hraw[:], in_=hid.rearrange("(p j) q -> p j q", j=PACK))
-        nc.sync.dma_start(out=tbcol[:], in_=tb.rearrange("o (k c) -> (o k) c", c=4))
         nc.sync.dma_start(out=words[:], in_=voc_words[0].rearrange("p n t -> p (n t)").bitcast(I32))
-        for g in range(4):
-            nc.scalar.dma_start(
-                out=scales[32 * g : 32 * g + 4, :].bitcast(I32),
-                in_=voc_scales[0, 4 * g : 4 * g + 4, :].bitcast(I32),
-            )
+        nc.sync.dma_start(out=tbcol[:], in_=tb.rearrange("o (k c) -> (o k) c", c=4))
 
-        ident = sb.tile([P, P], F32, name="ident")
-        make_identity(nc, ident[:])
-
-        kf = sb.tile([P, TERMS], F32, name="kf")
-        ke = sb.tile([P, TERMS], I32, name="ke")
-        pw = sb.tile([P, TERMS], I32, name="pw")
-        den = sb.tile([P, TERMS], F32, name="den")
-        cf = sb.tile([P, TERMS + 1], F32, name="cf")
-        nc.gpsimd.iota(kf[:], [[-1, TERMS]], base=TERMS, channel_multiplier=0, allow_small_or_imprecise_dtypes=True)
-        nc.gpsimd.iota(ke[:], [[-2, TERMS]], base=127 + 2 * TERMS, channel_multiplier=0)
-        nc.vector.tensor_scalar(pw[:], ke[:], 23, None, ALU.logical_shift_left)
-        nc.vector.tensor_tensor(den[:], kf[:], pw[:].bitcast(F32), ALU.mult)
-        nc.vector.reciprocal(cf[:, 0:TERMS], den[:])
-
-        hgrp = sb.tile([P, Q, PACK], BF16, name="hgrp", align_bytes=64)
-        hq = sb.tile([P, Q], U32, name="hq", align_bytes=64)
+        hgrp = sb.tile([P, Q, PACK], BF16, name="hgrp", tag="hgrp", align_bytes=64)
         hs = sb.tile([P, Q], U8, name="hs", align_bytes=64)
         nc.scalar.copy(hgrp[:], hraw[:].rearrange("p j q -> p q j"))
 
-        gs1 = sb.tile([P, NI], U8, name="gs1", align_bytes=64)
-        gw2 = sb.tile([P, NJ], U32, name="gw2", align_bytes=64)
+        gs2 = sb.tile([P, NJ], U8, name="gs2", align_bytes=64)
         gw1 = sb.tile([P, NI], U32, name="gw1", align_bytes=64)
         lfg = sb.tile([P, NJ], F32, name="lfg")
+
+        def gather_scales(plane, gathered, lst):
+            nc.vector.tensor_copy(gathered[:], scales[:].indirect(lst[:]))
+            for r in range(4):
+                nc.sync.dma_start(
+                    out=plane[r:P:32, :].bitcast(I32),
+                    in_=gathered[SC_ROW + r : SC_ROW + 16 : 4, :].bitcast(I32),
+                )
+
+        gather_scales(pl2, gs2, o2)
         nc.vector.tensor_copy(lfg[:], lf[:].indirect(o2[:]))
-        gs2 = sb.tile([P, NJ], U8, name="gs2", tag="lf", align_bytes=64)
-        nc.vector.tensor_copy(gs2[:], scales[:].indirect(o2[:]))
+        gs1 = sb.tile([P, NI], U8, name="gs1", tag="lf", align_bytes=64)
+        gather_scales(pl1, gs1, o1)
+        hq = sb.tile([P, Q], U32, name="hq", tag="scales", align_bytes=64)
         nc.vector.quantize_mx(out=hq[:].bitcast(FP8X4), scales=hs[:], in_=hgrp[:].rearrange("p q j -> p (q j)"))
-        nc.vector.tensor_copy(gs1[:], scales[:].indirect(o1[:]))
+        gw2 = sb.tile([P, NJ], U32, name="gw2", tag="hgrp", align_bytes=64)
         nc.vector.tensor_copy(gw2[:], words[:].bitcast(U32).indirect(o2[:]))
         nc.vector.tensor_copy(gw1[:], words[:].bitcast(U32).indirect(o1[:]))
 
-        lft = ps.tile([P, 4, P], F32, name="lft")
+        lft = ps.tile([P, 4, P], F32, name="lft", tag="turn")
         lfcol = sb.tile([P, 4], F32, name="lfcol")
         lfp = ps.tile([P, 4, P], F32, name="lfp")
-        lfb = sb.tile([P, NJ], F32, name="lfb")
+        lfb = sb.tile([P, NJ], F32, name="lfb", tag="lfb")
         for c in range(4):
             nc.tensor.transpose(lft[:, c, :], lfg[:, c * P : (c + 1) * P], ident[:])
         nc.scalar.copy(lfcol[:], lft[:, :, LF_ROW])
@@ -101,18 +108,18 @@ def tile_attend_sampledsum_kernel(tc, hid, voc_words, voc_scales, lfreq, tb, off
             nc.tensor.transpose(lfp[:, c, :], lfcol[:, c : c + 1].to_broadcast([P, P]), ident[:])
         nc.scalar.copy(lfb[:], lfp[:].rearrange("p c k -> p (c k)"))
 
-        tbp = ps.tile([P, 4, P], F32, name="tbp")
+        tbp = ps.tile([P, 4, P], F32, name="tbp", tag="turn")
         tbb = sb.tile([P, P, 4], F32, name="tbb")
         for c in range(4):
             nc.tensor.transpose(tbp[:, c, :], tbcol[:, c : c + 1].to_broadcast([P, P]), ident[:])
-        nc.scalar.copy(tbb[:], tbp[:].rearrange("p c k -> p k c"))
+        nc.scalar.activation(tbb[:], tbp[:].rearrange("p c k -> p k c"), ACT.Copy, bias=12.0 + math.log(MANT_VALUE / 4.0))
 
         pb = ps.tile([P, NJ], F32, name="pb")
         pa = ps.tile([P, NI], F32, name="pa")
         nc.tensor.matmul_mx(out=pb[:], lhsT=hq[:].bitcast(FP8X4), lhsT_scale=hs[:],
-                            rhs=gw2[:].bitcast(FP8X4), rhs_scale=gs2[:], start=True, stop=True)
+                            rhs=gw2[:].bitcast(FP8X4), rhs_scale=pl2[:], start=True, stop=True)
         nc.tensor.matmul_mx(out=pa[:], lhsT=hq[:].bitcast(FP8X4), lhsT_scale=hs[:],
-                            rhs=gw1[:].bitcast(FP8X4), rhs_scale=gs1[:], start=True, stop=True)
+                            rhs=gw1[:].bitcast(FP8X4), rhs_scale=pl1[:], start=True, stop=True)
 
         nr = sb.tile([P, NJ], F32, name="nr")
         negm = sb.tile([P, 1], F32, name="negm")
@@ -125,6 +132,13 @@ def tile_attend_sampledsum_kernel(tc, hid, voc_words, voc_scales, lfreq, tb, off
         at = sb.tile([P, NI], F32, name="at")
         nc.vector.scalar_tensor_tensor(at[:], pa[:], negm[:], tbb[:].rearrange("p k c -> p (k c)"), ALU.add, ALU.add)
 
+        pw = sb.tile([P, TERMS], I32, name="pw", tag="lfb")
+        den = sb.tile([P, TERMS], F32, name="den")
+        cf = sb.tile([P, TERMS + 1], F32, name="cf")
+        nc.vector.tensor_scalar(pw[:], ke[:], 23, None, ALU.logical_shift_left)
+        nc.vector.scalar_tensor_tensor(den[:], ke[:], -126.0, pw[:].bitcast(F32), ALU.add, ALU.mult)
+        nc.vector.reciprocal(cf[:, 0:TERMS], den[:])
+
         inv = sb.tile([P, 1], I32, name="inv")
         w = sb.tile([P, TERMS + 1], F32, name="w")
         hor = sb.tile([P, TERMS + 1], F32, name="hor")
@@ -133,6 +147,9 @@ def tile_attend_sampledsum_kernel(tc, hid, voc_words, voc_scales, lfreq, tb, off
         nc.vector.tensor_scalar(cf[:, TERMS : TERMS + 1], inv[:], float(-BITS_OF_ONE), math.log(2.0) / (1 << 23), ALU.add, ALU.mult)
         nc.vector.tensor_tensor_scan(hor[:], w[:], cf[:], 0.0, ALU.mult, ALU.add)
 
-        res = sb.tile([P, NI], F32, name="res")
-        nc.vector.tensor_scalar(res[:], at[:], hor[:, TERMS : TERMS + 1], 12.0 + math.log(MANT_VALUE / 4.0), ALU.add, ALU.add)
-        nc.sync.dma_start(out=out, in_=res[:])
+        resv = sb.tile([P, VCOLS], F32, name="resv")
+        ress = sb.tile([P, NI - VCOLS], F32, name="ress")
+        nc.vector.tensor_scalar(resv[:], at[:, 0:VCOLS], hor[:, TERMS : TERMS + 1], None, ALU.add)
+        nc.scalar.activation(ress[:], at[:, VCOLS:NI], ACT.Identity, bias=hor[:, TERMS : TERMS + 1])
+        nc.sync.dma_start(out=out[:, 0:VCOLS], in_=resv[:])
+        nc.scalar.dma_start(out=out[:, VCOLS:NI], in_=ress[:])

@@ -28,7 +28,7 @@ MANT_VALUE = 1.3125
 FLIP = (0x80000000 | EXP_MASK | MANT) - (1 << 32)
 BITS_OF_ONE = (0x80000000 | (127 << 23) | MANT) - (1 << 32)
 LF_ROW = P - 1
-SPLIT = 1600
+SPLIT = 1448
 SC_ROW = 48
 VCOLS = 320
 
@@ -42,7 +42,7 @@ def tile_attend_sampledsum_kernel(tc, hid, voc_words, voc_scales, lfreq, tb, off
         o2 = sb.tile([P, NJ // 16], U16, name="o2")
         o1 = sb.tile([P, NI // 16], U16, name="o1")
         words = sb.tile([P, T], I32, name="words", align_bytes=64)
-        scales = sb.tile([P, T], U8, name="scales", tag="scales", align_bytes=64)
+        scales = sb.tile([P, T], U8, name="scales", align_bytes=64)
         lf = sb.tile([P, T], F32, name="lf", tag="lf", align_bytes=64)
         hraw = sb.tile([P, PACK, Q], F32, name="hraw")
         tbcol = sb.tile([P, 4], F32, name="tbcol")
@@ -71,13 +71,13 @@ def tile_attend_sampledsum_kernel(tc, hid, voc_words, voc_scales, lfreq, tb, off
         nc.sync.dma_start(out=words[:], in_=voc_words[0].rearrange("p n t -> p (n t)").bitcast(I32))
         nc.sync.dma_start(out=tbcol[:], in_=tb.rearrange("o (k c) -> (o k) c", c=4))
 
-        hgrp = sb.tile([P, Q, PACK], BF16, name="hgrp", tag="hgrp", align_bytes=64)
+        hgrp = sb.tile([P, Q, PACK], BF16, name="hgrp", align_bytes=64)
         hs = sb.tile([P, Q], U8, name="hs", align_bytes=64)
         nc.scalar.copy(hgrp[:], hraw[:].rearrange("p j q -> p q j"))
 
         gs2 = sb.tile([P, NJ], U8, name="gs2", align_bytes=64)
         gw1 = sb.tile([P, NI], U32, name="gw1", align_bytes=64)
-        lfg = sb.tile([P, NJ], F32, name="lfg")
+        lfg = sb.tile([P, NJ], F32, name="lfg", tag="lfg", align_bytes=64)
 
         def gather_scales(plane, gathered, lst):
             nc.vector.tensor_copy(gathered[:], scales[:].indirect(lst[:]))
@@ -91,11 +91,6 @@ def tile_attend_sampledsum_kernel(tc, hid, voc_words, voc_scales, lfreq, tb, off
         nc.vector.tensor_copy(lfg[:], lf[:].indirect(o2[:]))
         gs1 = sb.tile([P, NI], U8, name="gs1", tag="lf", align_bytes=64)
         gather_scales(pl1, gs1, o1)
-        hq = sb.tile([P, Q], U32, name="hq", tag="scales", align_bytes=64)
-        nc.vector.quantize_mx(out=hq[:].bitcast(FP8X4), scales=hs[:], in_=hgrp[:].rearrange("p q j -> p (q j)"))
-        gw2 = sb.tile([P, NJ], U32, name="gw2", tag="hgrp", align_bytes=64)
-        nc.vector.tensor_copy(gw2[:], words[:].bitcast(U32).indirect(o2[:]))
-        nc.vector.tensor_copy(gw1[:], words[:].bitcast(U32).indirect(o1[:]))
 
         lft = ps.tile([P, 4, P], F32, name="lft", tag="turn")
         lfcol = sb.tile([P, 4], F32, name="lfcol")
@@ -103,6 +98,11 @@ def tile_attend_sampledsum_kernel(tc, hid, voc_words, voc_scales, lfreq, tb, off
         lfb = sb.tile([P, NJ], F32, name="lfb", tag="lfb")
         for c in range(4):
             nc.tensor.transpose(lft[:, c, :], lfg[:, c * P : (c + 1) * P], ident[:])
+        hq = sb.tile([P, Q], U32, name="hq", tag="lfg", align_bytes=64)
+        nc.vector.quantize_mx(out=hq[:].bitcast(FP8X4), scales=hs[:], in_=hgrp[:].rearrange("p q j -> p (q j)"))
+        gw2 = sb.tile([P, NJ], U32, name="gw2", align_bytes=64)
+        nc.vector.tensor_copy(gw2[:], words[:].bitcast(U32).indirect(o2[:]))
+        nc.vector.tensor_copy(gw1[:], words[:].bitcast(U32).indirect(o1[:]))
         nc.scalar.copy(lfcol[:], lft[:, :, LF_ROW])
         for c in range(4):
             nc.tensor.transpose(lfp[:, c, :], lfcol[:, c : c + 1].to_broadcast([P, P]), ident[:])

import math
from contextlib import ExitStack

import concourse.mybir as mybir
from concourse.masks import make_identity

D, T, NI, NJ, Q = 512, 4096, 512, 512, 128
P = 128
PACK = 4
FLOPS = 2 * Q * D * (NI + NJ)
BYTES = D * T + (D // 32) * T + 4 * D * Q + 4 * T + 4 * NI + 2 * 2 * P * 32 + 4 * Q * NI

F32 = mybir.dt.float32
BF16 = mybir.dt.bfloat16
I32 = mybir.dt.int32
U32 = mybir.dt.uint32
U16 = mybir.dt.uint16
U8 = mybir.dt.uint8
FP8X4 = mybir.dt.float8_e4m3fn_x4
ALU = mybir.AluOpType
ACT = mybir.ActivationFunctionType
AX = mybir.AxisListType

TERMS = 24
EXP_MASK = 0x7F800000
MANT = 0x280000
MANT_VALUE = 1.3125
FLIP = (0x80000000 | EXP_MASK | MANT) - (1 << 32)
BITS_OF_ONE = (0x80000000 | (127 << 23) | MANT) - (1 << 32)
LF_ROW = P - 1
SPLIT = 1448
SC_ROW = 48
VCOLS = 320


def tile_attend_sampledsum_kernel(tc, hid, voc_words, voc_scales, lfreq, tb, offs, offs2, out):
    nc = tc.nc
    with ExitStack() as ctx:
        sb = ctx.enter_context(tc.tile_pool(name="sb", bufs=1))
        ps = ctx.enter_context(tc.psum_pool(name="ps", bufs=1))

        o2 = sb.tile([P, NJ // 16], U16, name="o2")
        o1 = sb.tile([P, NI // 16], U16, name="o1")
        words = sb.tile([P, T], I32, name="words", align_bytes=64)
        scales = sb.tile([P, T], U8, name="scales", align_bytes=64)
        lf = sb.tile([P, T], F32, name="lf", tag="lf", align_bytes=64)
        hraw = sb.tile([P, PACK, Q], F32, name="hraw")
        tbcol = sb.tile([P, 4], F32, name="tbcol")

        scw = scales[:].bitcast(I32)
        ident = sb.tile([P, P], F32, name="ident")
        ke = sb.tile([P, TERMS], I32, name="ke")
        pl2 = sb.tile([P, NJ], U8, name="pl2", align_bytes=64)
        pl1 = sb.tile([P, NI], U8, name="pl1", align_bytes=64)
        nc.gpsimd.memset(scw[64:P, :], 0)
        nc.vector.memset(scw[0:SC_ROW, 0 : T // 4 - 1], 0)
        nc.vector.memset(scw[0:SC_ROW, T // 4 - 1 : T // 4], 0)
        nc.vector.memset(lf[0:LF_ROW, 0 : SPLIT - 1], 0.0)
        nc.vector.memset(lf[0:LF_ROW, SPLIT - 1 : SPLIT], 0.0)
        nc.gpsimd.memset(lf[0:LF_ROW, SPLIT:T], 0.0)
        make_identity(nc, ident[:])
        nc.gpsimd.memset(pl2[:].bitcast(I32), 0)
        nc.gpsimd.memset(pl1[:].bitcast(I32), 0)
        nc.gpsimd.iota(ke[:], [[-2, TERMS]], base=126 + 2 * TERMS, channel_multiplier=0)

        nc.sync.dma_start(o2[:], offs2)
        nc.sync.dma_start(out=scw[SC_ROW : SC_ROW + 16, :], in_=voc_scales[0].bitcast(I32))
        nc.sync.dma_start(out=hraw[:], in_=hid.rearrange("(p j) q -> p j q", j=PACK))
        nc.sync.dma_start(o1[:], offs)
        nc.sync.dma_start(out=lf[LF_ROW:P, :], in_=lfreq[0:1, :])
        nc.sync.dma_start(out=words[:], in_=voc_words[0].rearrange("p n t -> p (n t)").bitcast(I32))
        nc.sync.dma_start(out=tbcol[:], in_=tb.rearrange("o (k c) -> (o k) c", c=4))

        hgrp = sb.tile([P, Q, PACK], BF16, name="hgrp", align_bytes=64)
        hs = sb.tile([P, Q], U8, name="hs", align_bytes=64)
        nc.scalar.copy(hgrp[:], hraw[:].rearrange("p j q -> p q j"))

        gs2 = sb.tile([P, NJ], U8, name="gs2", align_bytes=64)
        gw1 = sb.tile([P, NI], U32, name="gw1", align_bytes=64)
        lfg = sb.tile([P, NJ], F32, name="lfg", tag="lfg", align_bytes=64)

        def gather_scales(plane, gathered, lst):
            nc.vector.tensor_copy(gathered[:], scales[:].indirect(lst[:]))
            for r in range(4):
                nc.sync.dma_start(
                    out=plane[r:P:32, :].bitcast(I32),
                    in_=gathered[SC_ROW + r : SC_ROW + 16 : 4, :].bitcast(I32),
                )

        gather_scales(pl2, gs2, o2)
        nc.vector.tensor_copy(lfg[:], lf[:].indirect(o2[:]))
        gs1 = sb.tile([P, NI], U8, name="gs1", tag="lf", align_bytes=64)
        gather_scales(pl1, gs1, o1)

        lft = ps.tile([P, 4, P], F32, name="lft", tag="turn")
        lfcol = sb.tile([P, 4], F32, name="lfcol")
        lfp = ps.tile([P, 4, P], F32, name="lfp")
        lfb = sb.tile([P, NJ], F32, name="lfb", tag="lfb")
        for c in range(4):
            nc.tensor.transpose(lft[:, c, :], lfg[:, c * P : (c + 1) * P], ident[:])
        hq = sb.tile([P, Q], U32, name="hq", tag="lfg", align_bytes=64)
        nc.vector.quantize_mx(out=hq[:].bitcast(FP8X4), scales=hs[:], in_=hgrp[:].rearrange("p q j -> p (q j)"))
        gw2 = sb.tile([P, NJ], U32, name="gw2", align_bytes=64)
        nc.vector.tensor_copy(gw2[:], words[:].bitcast(U32).indirect(o2[:]))
        nc.vector.tensor_copy(gw1[:], words[:].bitcast(U32).indirect(o1[:]))
        nc.scalar.copy(lfcol[:], lft[:, :, LF_ROW])
        for c in range(4):
            nc.tensor.transpose(lfp[:, c, :], lfcol[:, c : c + 1].to_broadcast([P, P]), ident[:])
        nc.scalar.copy(lfb[:], lfp[:].rearrange("p c k -> p (c k)"))

        tbp = ps.tile([P, 4, P], F32, name="tbp", tag="turn")
        tbb = sb.tile([P, P, 4], F32, name="tbb")
        for c in range(4):
            nc.tensor.transpose(tbp[:, c, :], tbcol[:, c : c + 1].to_broadcast([P, P]), ident[:])
        nc.scalar.activation(tbb[:], tbp[:].rearrange("p c k -> p k c"), ACT.Copy, bias=12.0 + math.log(MANT_VALUE / 4.0))

        pb = ps.tile([P, NJ], F32, name="pb")
        pa = ps.tile([P, NI], F32, name="pa")
        nc.tensor.matmul_mx(out=pb[:], lhsT=hq[:].bitcast(FP8X4), lhsT_scale=hs[:],
                            rhs=gw2[:].bitcast(FP8X4), rhs_scale=pl2[:], start=True, stop=True)
        nc.tensor.matmul_mx(out=pa[:], lhsT=hq[:].bitcast(FP8X4), lhsT_scale=hs[:],
                            rhs=gw1[:].bitcast(FP8X4), rhs_scale=pl1[:], start=True, stop=True)

        nr = sb.tile([P, NJ], F32, name="nr")
        negm = sb.tile([P, 1], F32, name="negm")
        ex = sb.tile([P, NJ], F32, name="ex")
        ssum = sb.tile([P, 1], F32, name="ssum")
        nc.vector.tensor_tensor(nr[:], lfb[:], pb[:], ALU.subtract)
        nc.vector.tensor_reduce(negm[:], nr[:], AX.X, ALU.min)
        nc.scalar.activation(ex[:], nr[:], ACT.Exp, bias=negm[:], scale=-1.0, accum_out=ssum[:])

        at = sb.tile([P, NI], F32, name="at")
        nc.vector.scalar_tensor_tensor(at[:], pa[:], negm[:], tbb[:].rearrange("p k c -> p (k c)"), ALU.add, ALU.add)

        pw = sb.tile([P, TERMS], I32, name="pw", tag="lfb")
        den = sb.tile([P, TERMS], F32, name="den")
        cf = sb.tile([P, TERMS + 1], F32, name="cf")
        nc.vector.tensor_scalar(pw[:], ke[:], 23, None, ALU.logical_shift_left)
        nc.vector.scalar_tensor_tensor(den[:], ke[:], -126.0, pw[:].bitcast(F32), ALU.add, ALU.mult)
        nc.vector.reciprocal(cf[:, 0:TERMS], den[:])

        inv = sb.tile([P, 1], I32, name="inv")
        w = sb.tile([P, TERMS + 1], F32, name="w")
        hor = sb.tile([P, TERMS + 1], F32, name="hor")
        nc.vector.tensor_scalar(inv[:], ssum[:].bitcast(I32), EXP_MASK, FLIP, ALU.bitwise_and, ALU.bitwise_xor)
        nc.vector.tensor_scalar(w[:], ssum[:].to_broadcast([P, TERMS + 1]), inv[:].bitcast(F32), 4.0, ALU.mult, ALU.add)
        nc.vector.tensor_scalar(cf[:, TERMS : TERMS + 1], inv[:], float(-BITS_OF_ONE), math.log(2.0) / (1 << 23), ALU.add, ALU.mult)
        nc.vector.tensor_tensor_scan(hor[:], w[:], cf[:], 0.0, ALU.mult, ALU.add)

        resv = sb.tile([P, VCOLS], F32, name="resv")
        ress = sb.tile([P, NI - VCOLS], F32, name="ress")
        nc.vector.tensor_scalar(resv[:], at[:, 0:VCOLS], hor[:, TERMS : TERMS + 1], None, ALU.add)
        nc.scalar.activation(ress[:], at[:, VCOLS:NI], ACT.Identity, bias=hor[:, TERMS : TERMS + 1])
        nc.sync.dma_start(out=out[:, 0:VCOLS], in_=resv[:])
        nc.scalar.dma_start(out=out[:, VCOLS:NI], in_=ress[:])
